import numpy as np
import ml_dtypes


def mxq(x, axis, fmt="e4m3"):
    dtype, down = {"e4m3": (ml_dtypes.float8_e4m3fn, 7), "e5m2": (ml_dtypes.float8_e5m2, 14)}[fmt]
    v = np.moveaxis(np.asarray(x, np.float32).astype(ml_dtypes.bfloat16).astype(np.float64), axis, -1)
    blocks = v.reshape(v.shape[:-1] + (-1, 32))
    amax = np.abs(blocks).max(-1, keepdims=True)
    byte = np.maximum(np.where(amax > 0, np.frexp(amax)[1] - 1 + 127, 0) - down, 1)
    scale = np.exp2(byte - 127.0)
    codes = (blocks / scale).astype(np.float32).astype(dtype).astype(np.float64)
    return np.moveaxis((codes * scale).reshape(v.shape), -1, axis)


WIDE = False


def mx_kscale(k):
    if not WIDE:
        return np.ones(k)
    levels = np.array([10, -10, 5, -5, 0])
    if k % 512:
        return np.exp2(np.random.permutation(np.resize(levels, k // 32))).repeat(32)
    a = np.empty((k // 512, 16))
    for p in range(k // 512):
        a[p, :8] = np.random.permutation(np.resize(levels, 8))
        for g in range(8):
            far = levels[np.abs(levels - a[p, g]) >= 10]
            a[p, g + 8] = far[np.random.randint(len(far))]
    return np.exp2(a.ravel()).repeat(32)


def f64(x):
    return np.asarray(x).astype(np.float64)


def striped(idx):
    return np.tile(np.asarray(idx).reshape(-1, 16).T, (8, 1)).astype(np.uint16)


def unstriped(offs):
    return offs[:16].T.reshape(-1).astype(np.int64)


E2M1 = np.array([0.0, 0.5, 1.0, 1.5, 2.0, 3.0, 4.0, 6.0, -0.0, -0.5, -1.0, -1.5, -2.0, -3.0, -4.0, -6.0])


def pack_weight(w, fmt):
    k, n = w.shape
    w = f64(np.asarray(w, np.float32).astype(ml_dtypes.bfloat16)).reshape(k // 32, 32, n)
    amax = np.abs(w).max(1)
    if fmt == "e4m3":
        byte = np.frexp(amax)[1] - 1 + 127 - 7
    else:
        mant, ex = np.frexp(amax / 6.0)
        byte = np.where(mant > 0.5, ex, ex - 1) + 127
    byte = np.clip(np.where(amax > 0, byte, 1), 1, 254)
    scaled = (w * np.exp2(127.0 - byte)[:, None, :]).reshape(k, n).astype(np.float32)
    by_word = np.ascontiguousarray(scaled.reshape(k // 512, 128, 4, n).transpose(0, 1, 3, 2))
    if fmt == "e4m3":
        words = by_word.astype(ml_dtypes.float8_e4m3fn).view(np.uint8)
    else:
        c = by_word.astype(ml_dtypes.float4_e2m1fn).view(np.uint8) & 0xF
        words = (c[..., 0::2] | (c[..., 1::2] << 4)).reshape(k // 512, 128, 2 * n)
    return np.ascontiguousarray(words), np.ascontiguousarray(byte.astype(np.uint8).reshape(k // 512, 16, n))


def unpack_weight(words, scales, fmt):
    g, _, n = scales.shape
    words = np.ascontiguousarray(words).reshape(g, 128, n, -1)
    if fmt == "e4m3":
        vals = words.view(ml_dtypes.float8_e4m3fn).astype(np.float64)
    else:
        nib = np.empty((g, 128, n, 4), np.uint8)
        nib[..., 0::2] = words & 0xF
        nib[..., 1::2] = words >> 4
        vals = E2M1[nib]
    vals = vals * np.repeat(np.exp2(scales.astype(np.float64) - 127.0), 8, axis=1)[..., None]
    return vals.transpose(0, 1, 3, 2).reshape(g * 512, n)


B, N, T, D, NQ = 1, 1024, 4096, 512, 128
SEG = 32


def setup_inputs():
    n = np.random.standard_normal
    pages = np.random.permutation(T // 32)[:B * N // 32]
    idx = (pages[:, None] * 32 + np.arange(32)[None, :]).reshape(-1)
    s = mx_kscale(D)[:, None]
    kp = pack_weight(n((D, T)) / s, "e4m3")
    return {
        "qT": (n((B, D, NQ)) * s * (1.00 / np.sqrt(D))).astype(np.float32),
        "k_words": kp[0],
        "k_scales": kp[1],
        "offs": striped(idx),
    }


def reference(qT, k_words, k_scales, offs):
    idx = unstriped(offs)
    pick = lambda x, which: x[:, which].reshape(x.shape[0], B, -1).transpose(1, 0, 2)
    k = unpack_weight(k_words, k_scales, "e4m3")
    kg = pick(k, idx)
    qq = mxq(f64(qT), 1, "e4m3")
    a = qq.transpose(0, 2, 1) @ kg
    m = np.max(a, axis=-1, keepdims=True)
    e = np.exp(a - m)
    l = np.sum(e, axis=-1, keepdims=True)
    y = e.reshape(B, NQ, N // SEG, SEG).sum(-1) / l
    return y

@@ -1,0 +1,127 @@
+from contextlib import ExitStack
+
+import concourse.mybir as mybir
+
+F32 = mybir.dt.float32
+BF16 = mybir.dt.bfloat16
+I32 = mybir.dt.int32
+U32 = mybir.dt.uint32
+U16 = mybir.dt.uint16
+U8 = mybir.dt.uint8
+FP8X4 = mybir.dt.float8_e4m3fn_x4
+ALU = mybir.AluOpType
+ACT = mybir.ActivationFunctionType
+AX = mybir.AxisListType
+
+P = 128
+PACK = 4
+D = 512
+NQ = 128
+T = 4096
+N = 1024
+SEG = 32
+PAGES = N // SEG
+HALF = 512
+CHUNK = 256
+CHUNKS = N // CHUNK
+
+FLOPS = 2 * D * NQ * N
+
+
+def tile_attend_page_mass_kernel(tc, qT, k_words, k_scales, offs, out):
+    nc = tc.nc
+    with ExitStack() as ctx:
+        sb = ctx.enter_context(tc.tile_pool(name="sb", bufs=1))
+        ps = ctx.enter_context(tc.psum_pool(name="ps", bufs=1))
+
+        offsets = sb.tile([P, N // 16], U16, name="offsets")
+        scale_pool = sb.tile([P, T // 4], I32, name="scale_pool", align_bytes=64)
+        word_pool = sb.tile([P, T], I32, name="word_pool", align_bytes=64)
+        q_raw = sb.tile([P, PACK, NQ], F32, name="q_raw")
+        q_bf = sb.tile([P, NQ, PACK], BF16, name="q_bf", align_bytes=64)
+        q_codes = sb.tile([P, NQ], U32, name="q_codes", align_bytes=64)
+        q_scales = sb.tile([P, NQ], U8, name="q_scales", align_bytes=64)
+        picked_scales = sb.tile([P, N], U8, name="picked_scales", align_bytes=64)
+        key_scales = sb.tile([P, N // 4], I32, name="key_scales", align_bytes=64)
+        warm_in = sb.tile([P, 1], F32, name="warm_in")
+        warm_out = sb.tile([P, 1], F32, name="warm_out")
+
+        nc.vector.memset(scale_pool[:], 0)
+        nc.sync.dma_start(offsets[:], offs)
+        nc.sync.dma_start(q_raw[:], qT[0].rearrange("(p t) q -> p t q", t=PACK))
+        nc.sync.dma_start(word_pool[:], k_words[0].rearrange("p n t -> p (n t)").bitcast(I32))
+        nc.scalar.dma_start(scale_pool[32:96:4, :], k_scales[0].bitcast(I32))
+        nc.vector.memset(warm_in[:], 0.0)
+        nc.scalar.activation(warm_out[:], warm_in[:], ACT.Exp)
+        nc.vector.memset(key_scales[:], 0)
+
+        nc.vector.tensor_copy(picked_scales[:], scale_pool[:].bitcast(U8).indirect(offsets[:]))
+        for r in range(4):
+            nc.scalar.dma_start(key_scales[r:P:32, :], picked_scales[:].bitcast(I32)[32 + 4 * r : 96 : 16, :])
+
+        nc.vector.tensor_copy(q_bf[:], q_raw[:].rearrange("p t q -> p q t"))
+        nc.vector.quantize_mx(
+            out=q_codes[:].bitcast(FP8X4), scales=q_scales[:], in_=q_bf[:].rearrange("p q t -> p (q t)")
+        )
+
+        keys = [sb.tile([P, HALF], U32, name=f"keys{h}", align_bytes=64) for h in range(N // HALF)]
+        for h in range(N // HALF):
+            cols = slice(h * HALF // 16, (h + 1) * HALF // 16)
+            nc.vector.tensor_copy(keys[h][:], word_pool[:].bitcast(U32).indirect(offsets[:, cols]))
+
+        neg_max = sb.tile([P, CHUNKS], F32, name="neg_max")
+        scores = [ps.tile([P, CHUNK], F32, name=f"scores{c}") for c in range(CHUNKS)]
+        for c in range(CHUNKS):
+            h, at = divmod(c * CHUNK, HALF)
+            nc.tensor.matmul_mx(
+                out=scores[c][:],
+                lhsT=q_codes[:].bitcast(FP8X4),
+                lhsT_scale=q_scales[:],
+                rhs=keys[h][:, at : at + CHUNK].bitcast(FP8X4),
+                rhs_scale=key_scales[:].bitcast(U8)[:, c * CHUNK : (c + 1) * CHUNK],
+                start=True,
+                stop=True,
+            )
+        for c in range(CHUNKS):
+            nc.vector.tensor_reduce(neg_max[:, c : c + 1], scores[c][:], AX.X, ALU.max, negate=True)
+
+        neg_row_max = sb.tile([P, 1], F32, name="neg_row_max")
+        nc.vector.tensor_reduce(neg_row_max[:], neg_max[:], AX.X, ALU.min)
+
+        chunk_sum = sb.tile([P, CHUNKS], F32, name="chunk_sum")
+        weights = [sb.tile([P, CHUNK], F32, name=f"weights{c}") for c in range(CHUNKS)]
+        rescale = sb.tile([P, CHUNKS], F32, name="rescale")
+        for c in range(CHUNKS):
+            nc.scalar.activation(
+                weights[c][:], scores[c][:], ACT.Exp, bias=neg_max[:, c : c + 1], accum_out=chunk_sum[:, c : c + 1]
+            )
+        nc.scalar.activation(rescale[:], neg_max[:], ACT.Exp, bias=neg_row_max[:], scale=-1.0)
+
+        page_sum = sb.tile([P, CHUNKS, CHUNK // SEG], F32, name="page_sum")
+        scaled_sum = sb.tile([P, CHUNKS], F32, name="scaled_sum")
+        row_sum = sb.tile([P, 1], F32, name="row_sum")
+        inv_sum = sb.tile([P, 1], F32, name="inv_sum")
+        result = sb.tile([P, CHUNKS, CHUNK // SEG], F32, name="result")
+
+        def sum_pages(c):
+            nc.vector.tensor_reduce(
+                page_sum[:, c, :], weights[c][:].rearrange("p (j i) -> p j i", i=SEG), AX.X, ALU.add
+            )
+
+        for c in range(CHUNKS - 2):
+            sum_pages(c)
+        nc.vector.scalar_tensor_tensor(
+            scaled_sum[:], chunk_sum[:], 1.0, rescale[:], ALU.mult, ALU.mult, accum_out=row_sum[:]
+        )
+        sum_pages(CHUNKS - 2)
+        nc.vector.reciprocal(inv_sum[:], row_sum[:])
+        sum_pages(CHUNKS - 1)
+        nc.vector.scalar_tensor_tensor(
+            result[:],
+            page_sum[:],
+            inv_sum[:],
+            rescale[:].unsqueeze(2).to_broadcast([P, CHUNKS, CHUNK // SEG]),
+            ALU.mult,
+            ALU.mult,
+        )
+        nc.sync.dma_start(out[0], result[:].rearrange("p c j -> p (c j)"))

@@ -49,17 +49,20 @@ def tile_attend_page_mass_kernel(tc, qT, k_words, k_scales, offs, out):
         nc.vector.memset(scale_pool[:], 0)
         nc.sync.dma_start(offsets[:], offs)
         nc.sync.dma_start(q_raw[:], qT[0].rearrange("(p t) q -> p t q", t=PACK))
-        nc.sync.dma_start(word_pool[:], k_words[0].rearrange("p n t -> p (n t)").bitcast(I32))
-        nc.scalar.dma_start(scale_pool[32:96:4, :], k_scales[0].bitcast(I32))
+        words = k_words[0].rearrange("p n t -> p (n t)").bitcast(I32)
+        nc.sync.dma_start(word_pool[:, 0:256], words[:, 0:256])
+        nc.sync.dma_start(scale_pool[32:96:4, :], k_scales[0].bitcast(I32))
+        for a, b in ((256, 1024), (1024, 2048), (2048, 3072), (3072, 4096)):
+            nc.sync.dma_start(word_pool[:, a:b], words[:, a:b])
         nc.vector.memset(warm_in[:], 0.0)
         nc.scalar.activation(warm_out[:], warm_in[:], ACT.Exp)
         nc.vector.memset(key_scales[:], 0)
+        nc.scalar.copy(q_bf[:], q_raw[:].rearrange("p t q -> p q t"))
 
         nc.vector.tensor_copy(picked_scales[:], scale_pool[:].bitcast(U8).indirect(offsets[:]))
         for r in range(4):
             nc.scalar.dma_start(key_scales[r:P:32, :], picked_scales[:].bitcast(I32)[32 + 4 * r : 96 : 16, :])
 
-        nc.vector.tensor_copy(q_bf[:], q_raw[:].rearrange("p t q -> p q t"))
         nc.vector.quantize_mx(
             out=q_codes[:].bitcast(FP8X4), scales=q_scales[:], in_=q_bf[:].rearrange("p q t -> p (q t)")
         )

@@ -47,22 +47,23 @@ def tile_attend_page_mass_kernel(tc, qT, k_words, k_scales, offs, out):
         warm_out = sb.tile([P, 1], F32, name="warm_out")
 
         nc.vector.memset(scale_pool[:], 0)
-        nc.sync.dma_start(offsets[:], offs)
-        nc.sync.dma_start(q_raw[:], qT[0].rearrange("(p t) q -> p t q", t=PACK))
         words = k_words[0].rearrange("p n t -> p (n t)").bitcast(I32)
-        nc.sync.dma_start(word_pool[:, 0:256], words[:, 0:256])
+        nc.sync.dma_start(word_pool[:, 0:512], words[:, 0:512])
+        nc.sync.dma_start(offsets[:], offs)
+        nc.sync.dma_start(word_pool[:, 512:768], words[:, 512:768])
         nc.sync.dma_start(scale_pool[32:96:4, :], k_scales[0].bitcast(I32))
-        for a, b in ((256, 1024), (1024, 2048), (2048, 3072), (3072, 4096)):
+        nc.sync.dma_start(q_raw[:], qT[0].rearrange("(p t) q -> p t q", t=PACK))
+        for a, b in ((768, 2048), (2048, 3072), (3072, 4096)):
             nc.sync.dma_start(word_pool[:, a:b], words[:, a:b])
         nc.vector.memset(warm_in[:], 0.0)
         nc.scalar.activation(warm_out[:], warm_in[:], ACT.Exp)
         nc.vector.memset(key_scales[:], 0)
-        nc.scalar.copy(q_bf[:], q_raw[:].rearrange("p t q -> p q t"))
 
         nc.vector.tensor_copy(picked_scales[:], scale_pool[:].bitcast(U8).indirect(offsets[:]))
         for r in range(4):
             nc.scalar.dma_start(key_scales[r:P:32, :], picked_scales[:].bitcast(I32)[32 + 4 * r : 96 : 16, :])
 
+        nc.scalar.copy(q_bf[:], q_raw[:].rearrange("p t q -> p q t"))
         nc.vector.quantize_mx(
             out=q_codes[:].bitcast(FP8X4), scales=q_scales[:], in_=q_bf[:].rearrange("p q t -> p (q t)")
         )

@@ -43,25 +43,21 @@ def tile_attend_page_mass_kernel(tc, qT, k_words, k_scales, offs, out):
         q_scales = sb.tile([P, NQ], U8, name="q_scales", align_bytes=64)
         picked_scales = sb.tile([P, N], U8, name="picked_scales", align_bytes=64)
         key_scales = sb.tile([P, N // 4], I32, name="key_scales", align_bytes=64)
-        warm_in = sb.tile([P, 1], F32, name="warm_in")
-        warm_out = sb.tile([P, 1], F32, name="warm_out")
 
         nc.vector.memset(scale_pool[:], 0)
         words = k_words[0].rearrange("p n t -> p (n t)").bitcast(I32)
         nc.sync.dma_start(word_pool[:, 0:512], words[:, 0:512])
         nc.sync.dma_start(offsets[:], offs)
-        nc.sync.dma_start(word_pool[:, 512:768], words[:, 512:768])
         nc.sync.dma_start(scale_pool[32:96:4, :], k_scales[0].bitcast(I32))
         nc.sync.dma_start(q_raw[:], qT[0].rearrange("(p t) q -> p t q", t=PACK))
-        for a, b in ((768, 2048), (2048, 3072), (3072, 4096)):
+        for a, b in ((512, 1024), (1024, 2048), (2048, 3072), (3072, 4096)):
             nc.sync.dma_start(word_pool[:, a:b], words[:, a:b])
-        nc.vector.memset(warm_in[:], 0.0)
-        nc.scalar.activation(warm_out[:], warm_in[:], ACT.Exp)
         nc.vector.memset(key_scales[:], 0)
 
         nc.vector.tensor_copy(picked_scales[:], scale_pool[:].bitcast(U8).indirect(offsets[:]))
         for r in range(4):
-            nc.scalar.dma_start(key_scales[r:P:32, :], picked_scales[:].bitcast(I32)[32 + 4 * r : 96 : 16, :])
+            queue = nc.sync if r % 2 else nc.scalar
+            queue.dma_start(key_scales[r:P:32, :], picked_scales[:].bitcast(I32)[32 + 4 * r : 96 : 16, :])
 
         nc.scalar.copy(q_bf[:], q_raw[:].rearrange("p t q -> p q t"))
         nc.vector.quantize_mx(

@@ -22,7 +22,8 @@ N = 1024
 SEG = 32
 PAGES = N // SEG
 HALF = 512
-CHUNK = 256
+CHUNK = 128
+RUN = 256
 CHUNKS = N // CHUNK
 
 FLOPS = 2 * D * NQ * N
@@ -89,36 +90,44 @@ def tile_attend_page_mass_kernel(tc, qT, k_words, k_scales, offs, out):
         nc.vector.tensor_reduce(neg_row_max[:], neg_max[:], AX.X, ALU.min)
 
         chunk_sum = sb.tile([P, CHUNKS], F32, name="chunk_sum")
-        weights = [sb.tile([P, CHUNK], F32, name=f"weights{c}") for c in range(CHUNKS)]
+        weights = [sb.tile([P, RUN], F32, name=f"weights{r}") for r in range(N // RUN)]
         rescale = sb.tile([P, CHUNKS], F32, name="rescale")
         for c in range(CHUNKS):
+            r, at = divmod(c * CHUNK, RUN)
             nc.scalar.activation(
-                weights[c][:], scores[c][:], ACT.Exp, bias=neg_max[:, c : c + 1], accum_out=chunk_sum[:, c : c + 1]
+                weights[r][:, at : at + CHUNK],
+                scores[c][:],
+                ACT.Exp,
+                bias=neg_max[:, c : c + 1],
+                accum_out=chunk_sum[:, c : c + 1],
             )
         nc.scalar.activation(rescale[:], neg_max[:], ACT.Exp, bias=neg_row_max[:], scale=-1.0)
 
-        page_sum = sb.tile([P, CHUNKS, CHUNK // SEG], F32, name="page_sum")
+        page_sum = sb.tile([P, PAGES], F32, name="page_sum")
         scaled_sum = sb.tile([P, CHUNKS], F32, name="scaled_sum")
         row_sum = sb.tile([P, 1], F32, name="row_sum")
         inv_sum = sb.tile([P, 1], F32, name="inv_sum")
         result = sb.tile([P, CHUNKS, CHUNK // SEG], F32, name="result")
 
-        def sum_pages(c):
+        def sum_pages(r):
             nc.vector.tensor_reduce(
-                page_sum[:, c, :], weights[c][:].rearrange("p (j i) -> p j i", i=SEG), AX.X, ALU.add
+                page_sum[:, r * RUN // SEG : (r + 1) * RUN // SEG],
+                weights[r][:].rearrange("p (j i) -> p j i", i=SEG),
+                AX.X,
+                ALU.add,
             )
 
-        for c in range(CHUNKS - 2):
-            sum_pages(c)
+        for r in range(N // RUN - 2):
+            sum_pages(r)
         nc.vector.scalar_tensor_tensor(
             scaled_sum[:], chunk_sum[:], 1.0, rescale[:], ALU.mult, ALU.mult, accum_out=row_sum[:]
         )
-        sum_pages(CHUNKS - 2)
+        sum_pages(N // RUN - 2)
         nc.vector.reciprocal(inv_sum[:], row_sum[:])
-        sum_pages(CHUNKS - 1)
+        sum_pages(N // RUN - 1)
         nc.vector.scalar_tensor_tensor(
             result[:],
-            page_sum[:],
+            page_sum[:].rearrange("p (c j) -> p c j", c=CHUNKS),
             inv_sum[:],
             rescale[:].unsqueeze(2).to_broadcast([P, CHUNKS, CHUNK // SEG]),
             ALU.mult,

@@ -70,7 +70,8 @@ def tile_attend_page_mass_kernel(tc, qT, k_words, k_scales, offs, out):
             cols = slice(h * HALF // 16, (h + 1) * HALF // 16)
             nc.vector.tensor_copy(keys[h][:], word_pool[:].bitcast(U32).indirect(offsets[:, cols]))
 
-        neg_max = sb.tile([P, CHUNKS], F32, name="neg_max")
+        page_sum = sb.tile([P, PAGES], F32, name="page_sum")
+        neg_max = page_sum[:, PAGES - CHUNKS :]
         scores = [ps.tile([P, CHUNK], F32, name=f"scores{c}") for c in range(CHUNKS)]
         for c in range(CHUNKS):
             h, at = divmod(c * CHUNK, HALF)
@@ -87,7 +88,7 @@ def tile_attend_page_mass_kernel(tc, qT, k_words, k_scales, offs, out):
             nc.vector.tensor_reduce(neg_max[:, c : c + 1], scores[c][:], AX.X, ALU.max, negate=True)
 
         neg_row_max = sb.tile([P, 1], F32, name="neg_row_max")
-        nc.vector.tensor_reduce(neg_row_max[:], neg_max[:], AX.X, ALU.min)
+        nc.vector.tensor_reduce(neg_row_max[:], neg_max, AX.X, ALU.min)
 
         chunk_sum = sb.tile([P, CHUNKS], F32, name="chunk_sum")
         weights = [sb.tile([P, RUN], F32, name=f"weights{r}") for r in range(N // RUN)]
@@ -101,9 +102,8 @@ def tile_attend_page_mass_kernel(tc, qT, k_words, k_scales, offs, out):
                 bias=neg_max[:, c : c + 1],
                 accum_out=chunk_sum[:, c : c + 1],
             )
-        nc.scalar.activation(rescale[:], neg_max[:], ACT.Exp, bias=neg_row_max[:], scale=-1.0)
+        nc.scalar.activation(rescale[:], neg_max, ACT.Exp, bias=neg_row_max[:], scale=-1.0)
 
-        page_sum = sb.tile([P, PAGES], F32, name="page_sum")
         scaled_sum = sb.tile([P, CHUNKS], F32, name="scaled_sum")
         row_sum = sb.tile([P, 1], F32, name="row_sum")
         inv_sum = sb.tile([P, 1], F32, name="inv_sum")
@@ -117,14 +117,13 @@ def tile_attend_page_mass_kernel(tc, qT, k_words, k_scales, offs, out):
                 ALU.add,
             )
 
-        for r in range(N // RUN - 2):
+        for r in range(N // RUN - 1):
             sum_pages(r)
         nc.vector.scalar_tensor_tensor(
             scaled_sum[:], chunk_sum[:], 1.0, rescale[:], ALU.mult, ALU.mult, accum_out=row_sum[:]
         )
-        sum_pages(N // RUN - 2)
-        nc.vector.reciprocal(inv_sum[:], row_sum[:])
         sum_pages(N // RUN - 1)
+        nc.vector.reciprocal(inv_sum[:], row_sum[:])
         nc.vector.scalar_tensor_tensor(
             result[:],
             page_sum[:].rearrange("p (c j) -> p c j", c=CHUNKS),

@@ -21,7 +21,7 @@ T = 4096
 N = 1024
 SEG = 32
 PAGES = N // SEG
-HALF = 512
+GATHERS = ((0, 3), (3, 6), (6, 8))
 CHUNK = 128
 RUN = 256
 CHUNKS = N // CHUNK
@@ -65,21 +65,22 @@ def tile_attend_page_mass_kernel(tc, qT, k_words, k_scales, offs, out):
             out=q_codes[:].bitcast(FP8X4), scales=q_scales[:], in_=q_bf[:].rearrange("p q t -> p (q t)")
         )
 
-        keys = [sb.tile([P, HALF], U32, name=f"keys{h}", align_bytes=64) for h in range(N // HALF)]
-        for h in range(N // HALF):
-            cols = slice(h * HALF // 16, (h + 1) * HALF // 16)
-            nc.vector.tensor_copy(keys[h][:], word_pool[:].bitcast(U32).indirect(offsets[:, cols]))
+        keys = []
+        for g, (first, last) in enumerate(GATHERS):
+            picked = sb.tile([P, (last - first) * CHUNK], U32, name=f"keys{g}", align_bytes=64)
+            cols = slice(first * CHUNK // 16, last * CHUNK // 16)
+            nc.vector.tensor_copy(picked[:], word_pool[:].bitcast(U32).indirect(offsets[:, cols]))
+            keys.extend(picked[:, c * CHUNK : (c + 1) * CHUNK] for c in range(last - first))
 
         page_sum = sb.tile([P, PAGES], F32, name="page_sum")
         neg_max = page_sum[:, PAGES - CHUNKS :]
         scores = [ps.tile([P, CHUNK], F32, name=f"scores{c}") for c in range(CHUNKS)]
         for c in range(CHUNKS):
-            h, at = divmod(c * CHUNK, HALF)
             nc.tensor.matmul_mx(
                 out=scores[c][:],
                 lhsT=q_codes[:].bitcast(FP8X4),
                 lhsT_scale=q_scales[:],
-                rhs=keys[h][:, at : at + CHUNK].bitcast(FP8X4),
+                rhs=keys[c].bitcast(FP8X4),
                 rhs_scale=key_scales[:].bitcast(U8)[:, c * CHUNK : (c + 1) * CHUNK],
                 start=True,
                 stop=True,

@@ -51,14 +51,13 @@ def tile_attend_page_mass_kernel(tc, qT, k_words, k_scales, offs, out):
         nc.sync.dma_start(offsets[:], offs)
         nc.sync.dma_start(scale_pool[32:96:4, :], k_scales[0].bitcast(I32))
         nc.sync.dma_start(q_raw[:], qT[0].rearrange("(p t) q -> p t q", t=PACK))
-        for a, b in ((512, 1024), (1024, 2048), (2048, 3072), (3072, 4096)):
+        for a, b in ((512, 2304), (2304, 4096)):
             nc.sync.dma_start(word_pool[:, a:b], words[:, a:b])
         nc.vector.memset(key_scales[:], 0)
 
         nc.vector.tensor_copy(picked_scales[:], scale_pool[:].bitcast(U8).indirect(offsets[:]))
         for r in range(4):
-            queue = nc.sync if r % 2 else nc.scalar
-            queue.dma_start(key_scales[r:P:32, :], picked_scales[:].bitcast(I32)[32 + 4 * r : 96 : 16, :])
+            nc.sync.dma_start(key_scales[r:P:32, :], picked_scales[:].bitcast(I32)[32 + 4 * r : 96 : 16, :])
 
         nc.scalar.copy(q_bf[:], q_raw[:].rearrange("p t q -> p q t"))
         nc.vector.quantize_mx(

@@ -57,7 +57,8 @@ def tile_attend_page_mass_kernel(tc, qT, k_words, k_scales, offs, out):
 
         nc.vector.tensor_copy(picked_scales[:], scale_pool[:].bitcast(U8).indirect(offsets[:]))
         for r in range(4):
-            nc.sync.dma_start(key_scales[r:P:32, :], picked_scales[:].bitcast(I32)[32 + 4 * r : 96 : 16, :])
+            queue = nc.scalar if r % 2 else nc.sync
+            queue.dma_start(key_scales[r:P:32, :], picked_scales[:].bitcast(I32)[32 + 4 * r : 96 : 16, :])
 
         nc.scalar.copy(q_bf[:], q_raw[:].rearrange("p t q -> p q t"))
         nc.vector.quantize_mx(

@@ -21,7 +21,7 @@ T = 4096
 N = 1024
 SEG = 32
 PAGES = N // SEG
-GATHERS = ((0, 3), (3, 6), (6, 8))
+GATHERS = ((0, 2), (2, 5), (5, 8))
 CHUNK = 128
 RUN = 256
 CHUNKS = N // CHUNK

@@ -58,7 +58,8 @@ def tile_attend_page_mass_kernel(tc, qT, k_words, k_scales, offs, out):
         nc.vector.tensor_copy(picked_scales[:], scale_pool[:].bitcast(U8).indirect(offsets[:]))
         for r in range(4):
             queue = nc.scalar if r % 2 else nc.sync
-            queue.dma_start(key_scales[r:P:32, :], picked_scales[:].bitcast(I32)[32 + 4 * r : 96 : 16, :])
+            for a, b in ((0, N // 4),) if r % 2 else ((0, 192), (192, N // 4)):
+                queue.dma_start(key_scales[r:P:32, a:b], picked_scales[:].bitcast(I32)[32 + 4 * r : 96 : 16, a:b])
 
         nc.scalar.copy(q_bf[:], q_raw[:].rearrange("p t q -> p q t"))
         nc.vector.quantize_mx(

@@ -49,7 +49,8 @@ def tile_attend_page_mass_kernel(tc, qT, k_words, k_scales, offs, out):
         words = k_words[0].rearrange("p n t -> p (n t)").bitcast(I32)
         nc.sync.dma_start(word_pool[:, 0:512], words[:, 0:512])
         nc.sync.dma_start(offsets[:], offs)
-        nc.sync.dma_start(scale_pool[32:96:4, :], k_scales[0].bitcast(I32))
+        for a, b in ((0, 384), (384, 768), (768, T // 4)):
+            nc.sync.dma_start(scale_pool[32:96:4, a:b], k_scales[0].bitcast(I32)[:, a:b])
         nc.sync.dma_start(q_raw[:], qT[0].rearrange("(p t) q -> p t q", t=PACK))
         for a, b in ((512, 2304), (2304, 4096)):
             nc.sync.dma_start(word_pool[:, a:b], words[:, a:b])

from contextlib import ExitStack

import concourse.mybir as mybir

F32 = mybir.dt.float32
BF16 = mybir.dt.bfloat16
I32 = mybir.dt.int32
U32 = mybir.dt.uint32
U16 = mybir.dt.uint16
U8 = mybir.dt.uint8
FP8X4 = mybir.dt.float8_e4m3fn_x4
ALU = mybir.AluOpType
ACT = mybir.ActivationFunctionType
AX = mybir.AxisListType

P = 128
PACK = 4
D = 512
NQ = 128
T = 4096
N = 1024
SEG = 32
PAGES = N // SEG
GATHERS = ((0, 2), (2, 5), (5, 8))
CHUNK = 128
RUN = 256
CHUNKS = N // CHUNK

FLOPS = 2 * D * NQ * N


def tile_attend_page_mass_kernel(tc, qT, k_words, k_scales, offs, out):
    nc = tc.nc
    with ExitStack() as ctx:
        sb = ctx.enter_context(tc.tile_pool(name="sb", bufs=1))
        ps = ctx.enter_context(tc.psum_pool(name="ps", bufs=1))

        offsets = sb.tile([P, N // 16], U16, name="offsets")
        scale_pool = sb.tile([P, T // 4], I32, name="scale_pool", align_bytes=64)
        word_pool = sb.tile([P, T], I32, name="word_pool", align_bytes=64)
        q_raw = sb.tile([P, PACK, NQ], F32, name="q_raw")
        q_bf = sb.tile([P, NQ, PACK], BF16, name="q_bf", align_bytes=64)
        q_codes = sb.tile([P, NQ], U32, name="q_codes", align_bytes=64)
        q_scales = sb.tile([P, NQ], U8, name="q_scales", align_bytes=64)
        picked_scales = sb.tile([P, N], U8, name="picked_scales", align_bytes=64)
        key_scales = sb.tile([P, N // 4], I32, name="key_scales", align_bytes=64)

        nc.vector.memset(scale_pool[:], 0)
        words = k_words[0].rearrange("p n t -> p (n t)").bitcast(I32)
        nc.sync.dma_start(word_pool[:, 0:512], words[:, 0:512])
        nc.sync.dma_start(offsets[:], offs)
        for a, b in ((0, 384), (384, 768), (768, T // 4)):
            nc.sync.dma_start(scale_pool[32:96:4, a:b], k_scales[0].bitcast(I32)[:, a:b])
        nc.sync.dma_start(q_raw[:], qT[0].rearrange("(p t) q -> p t q", t=PACK))
        for a, b in ((512, 2304), (2304, 4096)):
            nc.sync.dma_start(word_pool[:, a:b], words[:, a:b])
        nc.vector.memset(key_scales[:], 0)

        nc.vector.tensor_copy(picked_scales[:], scale_pool[:].bitcast(U8).indirect(offsets[:]))
        for r in range(4):
            queue = nc.scalar if r % 2 else nc.sync
            for a, b in ((0, N // 4),) if r % 2 else ((0, 192), (192, N // 4)):
                queue.dma_start(key_scales[r:P:32, a:b], picked_scales[:].bitcast(I32)[32 + 4 * r : 96 : 16, a:b])

        nc.scalar.copy(q_bf[:], q_raw[:].rearrange("p t q -> p q t"))
        nc.vector.quantize_mx(
            out=q_codes[:].bitcast(FP8X4), scales=q_scales[:], in_=q_bf[:].rearrange("p q t -> p (q t)")
        )

        keys = []
        for g, (first, last) in enumerate(GATHERS):
            picked = sb.tile([P, (last - first) * CHUNK], U32, name=f"keys{g}", align_bytes=64)
            cols = slice(first * CHUNK // 16, last * CHUNK // 16)
            nc.vector.tensor_copy(picked[:], word_pool[:].bitcast(U32).indirect(offsets[:, cols]))
            keys.extend(picked[:, c * CHUNK : (c + 1) * CHUNK] for c in range(last - first))

        page_sum = sb.tile([P, PAGES], F32, name="page_sum")
        neg_max = page_sum[:, PAGES - CHUNKS :]
        scores = [ps.tile([P, CHUNK], F32, name=f"scores{c}") for c in range(CHUNKS)]
        for c in range(CHUNKS):
            nc.tensor.matmul_mx(
                out=scores[c][:],
                lhsT=q_codes[:].bitcast(FP8X4),
                lhsT_scale=q_scales[:],
                rhs=keys[c].bitcast(FP8X4),
                rhs_scale=key_scales[:].bitcast(U8)[:, c * CHUNK : (c + 1) * CHUNK],
                start=True,
                stop=True,
            )
        for c in range(CHUNKS):
            nc.vector.tensor_reduce(neg_max[:, c : c + 1], scores[c][:], AX.X, ALU.max, negate=True)

        neg_row_max = sb.tile([P, 1], F32, name="neg_row_max")
        nc.vector.tensor_reduce(neg_row_max[:], neg_max, AX.X, ALU.min)

        chunk_sum = sb.tile([P, CHUNKS], F32, name="chunk_sum")
        weights = [sb.tile([P, RUN], F32, name=f"weights{r}") for r in range(N // RUN)]
        rescale = sb.tile([P, CHUNKS], F32, name="rescale")
        for c in range(CHUNKS):
            r, at = divmod(c * CHUNK, RUN)
            nc.scalar.activation(
                weights[r][:, at : at + CHUNK],
                scores[c][:],
                ACT.Exp,
                bias=neg_max[:, c : c + 1],
                accum_out=chunk_sum[:, c : c + 1],
            )
        nc.scalar.activation(rescale[:], neg_max, ACT.Exp, bias=neg_row_max[:], scale=-1.0)

        scaled_sum = sb.tile([P, CHUNKS], F32, name="scaled_sum")
        row_sum = sb.tile([P, 1], F32, name="row_sum")
        inv_sum = sb.tile([P, 1], F32, name="inv_sum")
        result = sb.tile([P, CHUNKS, CHUNK // SEG], F32, name="result")

        def sum_pages(r):
            nc.vector.tensor_reduce(
                page_sum[:, r * RUN // SEG : (r + 1) * RUN // SEG],
                weights[r][:].rearrange("p (j i) -> p j i", i=SEG),
                AX.X,
                ALU.add,
            )

        for r in range(N // RUN - 1):
            sum_pages(r)
        nc.vector.scalar_tensor_tensor(
            scaled_sum[:], chunk_sum[:], 1.0, rescale[:], ALU.mult, ALU.mult, accum_out=row_sum[:]
        )
        sum_pages(N // RUN - 1)
        nc.vector.reciprocal(inv_sum[:], row_sum[:])
        nc.vector.scalar_tensor_tensor(
            result[:],
            page_sum[:].rearrange("p (c j) -> p c j", c=CHUNKS),
            inv_sum[:],
            rescale[:].unsqueeze(2).to_broadcast([P, CHUNKS, CHUNK // SEG]),
            ALU.mult,
            ALU.mult,
        )
        nc.sync.dma_start(out[0], result[:].rearrange("p c j -> p (c j)"))
